import numpy as np
import ml_dtypes


def mxq(x, axis, fmt="e4m3"):
    dtype, down = {"e4m3": (ml_dtypes.float8_e4m3fn, 7), "e5m2": (ml_dtypes.float8_e5m2, 14)}[fmt]
    v = np.moveaxis(np.asarray(x, np.float32).astype(ml_dtypes.bfloat16).astype(np.float64), axis, -1)
    blocks = v.reshape(v.shape[:-1] + (-1, 32))
    amax = np.abs(blocks).max(-1, keepdims=True)
    byte = np.maximum(np.where(amax > 0, np.frexp(amax)[1] - 1 + 127, 0) - down, 1)
    scale = np.exp2(byte - 127.0)
    codes = (blocks / scale).astype(np.float32).astype(dtype).astype(np.float64)
    return np.moveaxis((codes * scale).reshape(v.shape), -1, axis)


WIDE = False


def mx_kscale(k):
    if not WIDE:
        return np.ones(k)
    levels = np.array([10, -10, 5, -5, 0])
    if k % 512:
        return np.exp2(np.random.permutation(np.resize(levels, k // 32))).repeat(32)
    a = np.empty((k // 512, 16))
    for p in range(k // 512):
        a[p, :8] = np.random.permutation(np.resize(levels, 8))
        for g in range(8):
            far = levels[np.abs(levels - a[p, g]) >= 10]
            a[p, g + 8] = far[np.random.randint(len(far))]
    return np.exp2(a.ravel()).repeat(32)


BF16 = ml_dtypes.bfloat16


def bf(x):
    return np.asarray(x, np.float32).astype(BF16)


def f64(x):
    return np.asarray(x).astype(np.float64)


E2M1 = np.array([0.0, 0.5, 1.0, 1.5, 2.0, 3.0, 4.0, 6.0, -0.0, -0.5, -1.0, -1.5, -2.0, -3.0, -4.0, -6.0])


def pack_weight(w, fmt):
    k, n = w.shape
    w = f64(bf(w)).reshape(k // 32, 32, n)
    amax = np.abs(w).max(1)
    if fmt == "e4m3":
        byte = np.frexp(amax)[1] - 1 + 127 - 7
    else:
        mant, ex = np.frexp(amax / 6.0)
        byte = np.where(mant > 0.5, ex, ex - 1) + 127
    byte = np.clip(np.where(amax > 0, byte, 1), 1, 254)
    scaled = (w * np.exp2(127.0 - byte)[:, None, :]).reshape(k, n).astype(np.float32)
    by_word = np.ascontiguousarray(scaled.reshape(k // 512, 128, 4, n).transpose(0, 1, 3, 2))
    if fmt == "e4m3":
        words = by_word.astype(ml_dtypes.float8_e4m3fn).view(np.uint8)
    else:
        c = by_word.astype(ml_dtypes.float4_e2m1fn).view(np.uint8) & 0xF
        words = c[..., 0::2] | (c[..., 1::2] << 4)
    return np.ascontiguousarray(words), np.ascontiguousarray(byte.astype(np.uint8).reshape(k // 512, 16, n))


def unpack_weight(words, scales, fmt):
    g, p, n, _ = words.shape
    if fmt == "e4m3":
        vals = np.ascontiguousarray(words).view(ml_dtypes.float8_e4m3fn).astype(np.float64)
    else:
        nib = np.empty((g, p, n, 4), np.uint8)
        nib[..., 0::2] = words & 0xF
        nib[..., 1::2] = words >> 4
        vals = E2M1[nib]
    vals = vals * np.repeat(np.exp2(scales.astype(np.float64) - 127.0), 8, axis=1)[..., None]
    return vals.transpose(0, 1, 3, 2).reshape(g * 512, n)
def pack4(w):
    words, scales = pack_weight(w, "e2m1")
    return words.reshape(words.shape[0], 128, -1), scales


def unpack4(words, scales):
    return unpack_weight(words.reshape(words.shape[0], 128, -1, 2), scales, "e2m1")


V, P, KA, KB, H, N = 3, 512, 512, 1024, 1024, 512


def setup_inputs():
    sa, sb, t = mx_kscale(KA), mx_kscale(KB), mx_kscale(H)
    w_feat = np.random.standard_normal((KB, H)) / np.sqrt(KA + KB) / sb[:, None] * t
    w_val = np.random.standard_normal((H, N)) / np.sqrt(H) / t[:, None]
    w_dir = np.random.standard_normal((H, N)) / np.sqrt(V * H) / t[:, None]
    w_feat_words, w_feat_scales = pack4(w_feat)
    w_val_words, w_val_scales = pack4(w_val)
    w_dir_words, w_dir_scales = pack4(w_dir)
    return {"x_geo": bf(np.random.standard_normal((V * P, KA)) * sa),
            "x_feat": bf(np.random.standard_normal((V * P, KB)) * sb),
            "w_geo": bf(np.random.standard_normal((KA, H)) / np.sqrt(KA + KB) / sa[:, None] * t),
            "w_feat_words": w_feat_words, "w_feat_scales": w_feat_scales,
            "gate": bf(1 + 0.3 * np.random.standard_normal((P, H))),
            "w_val_words": w_val_words, "w_val_scales": w_val_scales,
            "w_dir_words": w_dir_words, "w_dir_scales": w_dir_scales}


def reference(x_geo, x_feat, w_geo, w_feat_words, w_feat_scales, gate, w_val_words, w_val_scales, w_dir_words, w_dir_scales):
    z = ((mxq(f64(x_geo), 1, "e4m3") @ mxq(f64(w_geo), 0, "e4m3"))
         + (mxq(f64(x_feat), 1, "e4m3") @ unpack4(w_feat_words, w_feat_scales)))
    h = z.reshape(V, P, H) * f64(gate)
    hq = mxq(h.reshape(V * P, H), 1, "e4m3")
    feat = (hq @ unpack4(w_val_words, w_val_scales)).reshape(V, P, N)
    dirn = (hq @ unpack4(w_dir_words, w_dir_scales)).reshape(V, P, N)
    neg = np.minimum((feat * dirn).sum(axis=0), 0.0)
    return feat - neg * dirn

@@ -1,0 +1,312 @@
+from contextlib import ExitStack
+
+import concourse.mybir as mybir
+from concourse.masks import make_identity
+
+F32 = mybir.dt.float32
+BF16 = mybir.dt.bfloat16
+U32 = mybir.dt.uint32
+I32 = mybir.dt.int32
+U8 = mybir.dt.uint8
+FP8X4 = mybir.dt.float8_e4m3fn_x4
+FP4X4 = mybir.dt.float4_e2m1fn_x4
+ALU = mybir.AluOpType
+
+V, POINTS, KA, KB, H, N = 3, 512, 512, 1024, 1024, 512
+P = 128
+BANK = 512
+TILES = V * POINTS // P
+AHEAD = 3
+
+FLOPS = 2 * V * POINTS * (KA + KB) * H + 2 * 2 * V * POINTS * H * N
+
+
+def tile_gated_vector_neuron_relu_s3_kernel(
+    tc, x_geo, x_feat, w_geo, w_feat_words, w_feat_scales, gate,
+    w_val_words, w_val_scales, w_dir_words, w_dir_scales, out,
+):
+    nc = tc.nc
+    with ExitStack() as ctx:
+        ctx.enter_context(tc.manual_schedule())
+        keep = ctx.enter_context(tc.tile_pool(name="keep", bufs=1))
+        work = ctx.enter_context(tc.tile_pool(name="work", bufs=2))
+        psum = ctx.enter_context(tc.psum_pool(name="psum", bufs=8))
+
+        def bank():
+            return psum.tile([P, BANK], F32, name="bank", tag="bank")
+
+        wf = keep.tile([P, 2, 2 * H], U8, name="wf", align_bytes=256)
+        wf_s = keep.tile([P, 2, H], U8, name="wf_s", align_bytes=256)
+        wv = keep.tile([P, 2, 2 * N], U8, name="wv", align_bytes=256)
+        wv_s = keep.tile([P, 2, N], U8, name="wv_s", align_bytes=256)
+        wd = keep.tile([P, 2, 2 * N], U8, name="wd", align_bytes=256)
+        wd_s = keep.tile([P, 2, N], U8, name="wd_s", align_bytes=256)
+        wg_raw = [keep.tile([P, 4, BANK], BF16, name=f"wg_raw{h}", align_bytes=256) for h in range(2)]
+        x_sb = [keep.tile([P, V, KB + KA], BF16, name=f"x{m}", align_bytes=256) for m in range(POINTS // P)]
+        gate_sb = [keep.tile([P, H], BF16, name=f"gate{m}", align_bytes=256) for m in range(POINTS // P)]
+
+        def load_x(m, v0, v1):
+            for x, cols in ((x_feat, slice(0, KB)), (x_geo, slice(KB, KB + KA))):
+                rows = x.rearrange("(v q) k -> q v k", v=V)
+                nc.sync.dma_start(out=x_sb[m][:, v0:v1, cols], in_=rows[m * P:(m + 1) * P, v0:v1, :])
+
+        def load_gate(m):
+            nc.sync.dma_start(out=gate_sb[m][:], in_=gate[m * P:(m + 1) * P, :])
+
+        def load_words(tile, words):
+            nc.sync.dma_start(out=tile[:].bitcast(I32), in_=words.bitcast(I32).rearrange("g p b -> p g b"))
+
+        def load_scales(queue, tile, scales):
+            src = scales.bitcast(I32)
+            for q in range(4):
+                queue.dma_start(
+                    out=tile[32 * q:32 * q + 4, :, :].bitcast(I32),
+                    in_=src[:, 4 * q:4 * q + 4, :].rearrange("g q n -> q g n"),
+                )
+
+        def load_wg(h):
+            nc.sync.dma_start(
+                out=wg_raw[h][:],
+                in_=w_geo.rearrange("(p j) c -> p j c", j=4)[:, :, h * BANK:(h + 1) * BANK],
+            )
+
+        for plane in (wf_s, wv_s, wd_s):
+            nc.vector.memset(plane[:].bitcast(I32), 0)
+        load_x(0, 0, 1)
+        load_scales(nc.scalar, wf_s, w_feat_scales)
+        load_words(wf, w_feat_words)
+        load_x(0, 1, 2)
+        load_wg(0)
+        load_wg(1)
+        load_gate(0)
+        load_x(0, 2, 3)
+        load_words(wv, w_val_words)
+        load_words(wd, w_dir_words)
+        load_scales(nc.sync, wv_s, w_val_scales)
+        load_scales(nc.sync, wd_s, w_dir_scales)
+        for m in range(1, POINTS // P):
+            load_x(m, 0, V)
+            load_gate(m)
+
+        ident = keep.tile([P, P], F32, name="ident")
+        make_identity(nc, ident[:])
+
+        xq, xs, xg = {}, {}, {}
+        xbank = {}
+
+        def x_transpose(i, passes):
+            b = bank()
+            words = x_sb[i // V][:, i % V, :].bitcast(F32)
+            slot = 0
+            for g in passes:
+                for u in range(2):
+                    nc.tensor.transpose(b[:, slot * P:(slot + 1) * P], words[:, 256 * g + u:256 * (g + 1):2], ident[:])
+                    slot += 1
+            xbank[i, passes] = b
+
+        def x_copy(i, passes):
+            if i not in xg:
+                xg[i] = work.tile([P, 3 * 4 * P], BF16, name="xg", tag="xg", bufs=3, align_bytes=256)
+            n = len(passes)
+            c0 = passes[0] * 4 * P
+            dst = xg[i][:, c0:c0 + n * 4 * P].bitcast(F32).rearrange("p (g r u) -> p g r u", g=n, u=2)
+            src = xbank[i, passes][:, 0:n * 2 * P].rearrange("p (g u r) -> p g r u", g=n, u=2)
+            nc.scalar.copy(out=dst, in_=src)
+
+        def x_quant(i, passes):
+            if i not in xq:
+                xq[i] = work.tile([P, 3 * P], U32, name="xq", tag="xq", bufs=AHEAD + 2, align_bytes=256)
+                xs[i] = work.tile([P, 3 * P], U8, name="xs", tag="xs", bufs=AHEAD + 2, align_bytes=256)
+            n = len(passes)
+            c0 = passes[0] * P
+            nc.vector.quantize_mx(
+                out=xq[i][:, c0:c0 + n * P].bitcast(FP8X4),
+                scales=xs[i][:, c0:c0 + n * P],
+                in_=xg[i][:, 4 * c0:4 * (c0 + n * P)],
+            )
+
+        FEAT, GEO = (0, 1), (2,)
+
+        wg_codes = keep.tile([P, H], U32, name="wg_codes", align_bytes=256)
+        wg_scales = keep.tile([P, H], U8, name="wg_scales", align_bytes=256)
+        wg_grp = [keep.tile([P, BANK, 4], BF16, name=f"wg_grp{h}", align_bytes=256) for h in range(2)]
+
+        def wg_copy(h):
+            nc.vector.tensor_copy(
+                out=wg_grp[h][:].rearrange("p (c i) t -> p c t i", i=4),
+                in_=wg_raw[h][:].rearrange("p t (c i) -> p c t i", i=4),
+            )
+
+        def wg_quant(h):
+            cols = slice(h * BANK, (h + 1) * BANK)
+            nc.vector.quantize_mx(
+                out=wg_codes[:, cols].bitcast(FP8X4), scales=wg_scales[:, cols],
+                in_=wg_grp[h][:].rearrange("p c t -> p (c t)"),
+            )
+
+        z = {}
+
+        def lift(i, h, parts):
+            cols = slice(h * BANK, (h + 1) * BANK)
+            if (i, h) not in z:
+                z[i, h] = bank()
+            for s in parts:
+                if s < 2:
+                    rhs = wf[:, s, 2 * h * BANK:2 * (h + 1) * BANK].bitcast(FP4X4)
+                    rhs_scale = wf_s[:, s, cols]
+                else:
+                    rhs = wg_codes[:, cols].bitcast(FP8X4)
+                    rhs_scale = wg_scales[:, cols]
+                nc.tensor.matmul_mx(
+                    out=z[i, h][:],
+                    lhsT=xq[i][:, s * P:(s + 1) * P].bitcast(FP8X4),
+                    lhsT_scale=xs[i][:, s * P:(s + 1) * P],
+                    rhs=rhs, rhs_scale=rhs_scale,
+                    start=(s == 0), stop=(s == 2),
+                )
+
+        hsb, hbank, hg, hq, hs = {}, {}, {}, {}, {}
+
+        def gate_mul(i, h):
+            if i not in hsb:
+                hsb[i] = work.tile([P, H], BF16, name="hsb", tag="hsb", bufs=2, align_bytes=256)
+            cols = slice(h * BANK, (h + 1) * BANK)
+            nc.vector.tensor_tensor(
+                out=hsb[i][:, cols].rearrange("r (u p e) -> r u p e", u=2, e=2),
+                in0=z[i, h][:].rearrange("r (p u e) -> r u p e", u=2, e=2),
+                in1=gate_sb[i // V][:, cols].rearrange("r (p u e) -> r u p e", u=2, e=2),
+                op=ALU.mult,
+            )
+
+        def h_transpose(i):
+            hbank[i] = bank()
+            words = hsb[i][:].bitcast(F32)
+            for s in range(4):
+                nc.tensor.transpose(hbank[i][:, s * P:(s + 1) * P], words[:, s * P:(s + 1) * P], ident[:])
+
+        def h_copy(i):
+            hg[i] = work.tile([P, 2 * 4 * P], BF16, name="hg", tag="hg", bufs=2, align_bytes=256)
+            nc.scalar.copy(
+                out=hg[i][:].bitcast(F32).rearrange("p (g r u) -> p g r u", g=2, u=2),
+                in_=hbank[i][:].rearrange("p (g u r) -> p g r u", g=2, u=2),
+            )
+
+        def h_quant(i):
+            hq[i] = work.tile([P, 2 * P], U32, name="hq", tag="hq", bufs=2, align_bytes=256)
+            hs[i] = work.tile([P, 2 * P], U8, name="hs", tag="hs", bufs=2, align_bytes=256)
+            nc.vector.quantize_mx(out=hq[i][:].bitcast(FP8X4), scales=hs[i][:], in_=hg[i][:])
+
+        fbank, dbank, fsb, dsb, prod, summ, qt = {}, {}, {}, {}, {}, {}, {}
+
+        def project(i, w, w_s, banks):
+            banks[i] = bank()
+            for g in range(2):
+                nc.tensor.matmul_mx(
+                    out=banks[i][:],
+                    lhsT=hq[i][:, g * P:(g + 1) * P].bitcast(FP8X4),
+                    lhsT_scale=hs[i][:, g * P:(g + 1) * P],
+                    rhs=w[:, g, :].bitcast(FP4X4), rhs_scale=w_s[:, g, :],
+                    start=(g == 0), stop=(g == 1),
+                )
+
+        def f_copy(i):
+            fsb[i] = work.tile([P, N], F32, name="fsb", tag=f"f{i % V}", bufs=2)
+            nc.scalar.copy(out=fsb[i][:], in_=fbank[i][:])
+
+        def d_copy(i):
+            dsb[i] = work.tile([P, N], F32, name="dsb", tag=f"d{i % V}", bufs=2)
+            nc.scalar.copy(out=dsb[i][:], in_=dbank[i][:])
+
+        def product(i):
+            prod[i] = work.tile([P, N], F32, name="prod", tag="prod", bufs=3)
+            nc.vector.tensor_tensor(out=prod[i][:], in0=dbank[i][:], in1=fsb[i][:], op=ALU.mult)
+
+        def inner_sum(i):
+            m, v = divmod(i, V)
+            if v == 0:
+                return
+            left = prod[i - 1] if v == 1 else summ[m]
+            summ[m] = work.tile([P, N], F32, name="summ", tag="summ", bufs=3)
+            nc.vector.tensor_tensor(out=summ[m][:], in0=left[:], in1=prod[i][:], op=ALU.add)
+
+        def correction(i):
+            qt[i] = work.tile([P, N], F32, name="qt", tag="qt", bufs=3)
+            nc.vector.scalar_tensor_tensor(
+                out=qt[i][:], in0=summ[i // V][:], scalar=0.0, in1=dsb[i][:], op0=ALU.min, op1=ALU.mult,
+            )
+
+        def finish(i):
+            m, v = divmod(i, V)
+            res = work.tile([P, N], F32, name="res", tag="res", bufs=3)
+            nc.vector.tensor_tensor(out=res[:], in0=fsb[i][:], in1=qt[i][:], op=ALU.subtract)
+            nc.sync.dma_start(out=out[v, m * P:(m + 1) * P, :], in_=res[:])
+
+        for i in range(2):
+            x_transpose(i, FEAT)
+            x_transpose(i, GEO)
+            x_copy(i, FEAT)
+            x_copy(i, GEO)
+            x_quant(i, FEAT)
+            x_quant(i, GEO)
+        for i in range(2):
+            lift(i, 0, (0, 1))
+            lift(i, 1, (0, 1))
+        wg_copy(0)
+        wg_copy(1)
+        wg_quant(0)
+        lift(0, 0, (2,))
+        wg_quant(1)
+        lift(0, 1, (2,))
+        gate_mul(0, 0)
+        gate_mul(0, 1)
+        x_transpose(2, FEAT)
+        x_transpose(2, GEO)
+        x_copy(2, FEAT)
+        x_copy(2, GEO)
+        x_quant(2, FEAT)
+        x_quant(2, GEO)
+
+        for i in range(TILES):
+            j = i + AHEAD
+            if j < TILES:
+                x_transpose(j, FEAT)
+            h_transpose(i)
+            if j < TILES:
+                x_transpose(j, GEO)
+                x_copy(j, FEAT)
+            h_copy(i)
+            if j < TILES:
+                x_copy(j, GEO)
+            h_quant(i)
+            if i > 0:
+                product(i - 1)
+                d_copy(i - 1)
+            if i + 1 < TILES:
+                lift(i + 1, 0, (2,) if i == 0 else (0, 1, 2))
+                gate_mul(i + 1, 0)
+            if i > 0:
+                inner_sum(i - 1)
+            if i + 1 < TILES:
+                lift(i + 1, 1, (2,) if i == 0 else (0, 1, 2))
+                gate_mul(i + 1, 1)
+            if i >= V:
+                correction(i - V)
+            if j < TILES:
+                x_quant(j, FEAT)
+                x_quant(j, GEO)
+            if i >= V:
+                finish(i - V)
+            project(i, wv, wv_s, fbank)
+            project(i, wd, wd_s, dbank)
+            f_copy(i)
+
+        last = TILES - 1
+        product(last)
+        d_copy(last)
+        inner_sum(last)
+        correction(last - 2)
+        correction(last - 1)
+        finish(last - 2)
+        correction(last)
+        finish(last - 1)
+        finish(last)

@@ -11,6 +11,7 @@ U8 = mybir.dt.uint8
 FP8X4 = mybir.dt.float8_e4m3fn_x4
 FP4X4 = mybir.dt.float4_e2m1fn_x4
 ALU = mybir.AluOpType
+ACT = mybir.ActivationFunctionType
 
 V, POINTS, KA, KB, H, N = 3, 512, 512, 1024, 1024, 512
 P = 128
@@ -73,18 +74,22 @@ def tile_gated_vector_neuron_relu_s3_kernel(
         for plane in (wf_s, wv_s, wd_s):
             nc.vector.memset(plane[:].bitcast(I32), 0)
         load_x(0, 0, 1)
-        load_scales(nc.scalar, wf_s, w_feat_scales)
+        load_scales(nc.sync, wf_s, w_feat_scales)
         load_words(wf, w_feat_words)
         load_x(0, 1, 2)
         load_wg(0)
         load_wg(1)
         load_gate(0)
         load_x(0, 2, 3)
+        load_x(1, 0, 1)
         load_words(wv, w_val_words)
         load_words(wd, w_dir_words)
-        load_scales(nc.sync, wv_s, w_val_scales)
-        load_scales(nc.sync, wd_s, w_dir_scales)
-        for m in range(1, POINTS // P):
+        load_scales(nc.gpsimd, wv_s, w_val_scales)
+        load_scales(nc.gpsimd, wd_s, w_dir_scales)
+        load_x(1, 1, 2)
+        load_gate(1)
+        load_x(1, 2, 3)
+        for m in range(2, POINTS // P):
             load_x(m, 0, V)
             load_gate(m)
 
@@ -94,13 +99,25 @@ def tile_gated_vector_neuron_relu_s3_kernel(
         xq, xs, xg = {}, {}, {}
         xbank = {}
 
+        xr = {}
+
+        def x_reorder(i):
+            xr[i] = work.tile([P, KB + KA], BF16, name="xr", tag="xr", bufs=2, align_bytes=256)
+            nc.scalar.copy(
+                out=xr[i][:].bitcast(F32).rearrange("p (g u w) -> p g u w", g=3, u=2),
+                in_=x_sb[i // V][:, i % V, :].bitcast(F32).rearrange("p (g w u) -> p g u w", g=3, u=2),
+            )
+
         def x_transpose(i, passes):
             b = bank()
-            words = x_sb[i // V][:, i % V, :].bitcast(F32)
             slot = 0
             for g in passes:
                 for u in range(2):
-                    nc.tensor.transpose(b[:, slot * P:(slot + 1) * P], words[:, 256 * g + u:256 * (g + 1):2], ident[:])
+                    if i in xr:
+                        words = xr[i][:].bitcast(F32)[:, 256 * g + 128 * u:256 * g + 128 * (u + 1)]
+                    else:
+                        words = x_sb[i // V][:, i % V, :].bitcast(F32)[:, 256 * g + u:256 * (g + 1):2]
+                    nc.tensor.transpose(b[:, slot * P:(slot + 1) * P], words, ident[:])
                     slot += 1
             xbank[i, passes] = b
 
@@ -132,10 +149,12 @@ def tile_gated_vector_neuron_relu_s3_kernel(
         wg_grp = [keep.tile([P, BANK, 4], BF16, name=f"wg_grp{h}", align_bytes=256) for h in range(2)]
 
         def wg_copy(h):
-            nc.vector.tensor_copy(
-                out=wg_grp[h][:].rearrange("p (c i) t -> p c t i", i=4),
-                in_=wg_raw[h][:].rearrange("p t (c i) -> p c t i", i=4),
-            )
+            half = BANK // 2
+            for copy, c0 in ((nc.vector.tensor_copy, 0), (nc.scalar.copy, half)):
+                copy(
+                    out=wg_grp[h][:, c0:c0 + half, :].rearrange("p (c i) t -> p c t i", i=4),
+                    in_=wg_raw[h][:, :, c0:c0 + half].rearrange("p t (c i) -> p c t i", i=4),
+                )
 
         def wg_quant(h):
             cols = slice(h * BANK, (h + 1) * BANK)
@@ -169,7 +188,7 @@ def tile_gated_vector_neuron_relu_s3_kernel(
 
         def gate_mul(i, h):
             if i not in hsb:
-                hsb[i] = work.tile([P, H], BF16, name="hsb", tag="hsb", bufs=2, align_bytes=256)
+                hsb[i] = work.tile([P, H], BF16, name="hsb", tag="hsb", bufs=4, align_bytes=256)
             cols = slice(h * BANK, (h + 1) * BANK)
             nc.vector.tensor_tensor(
                 out=hsb[i][:, cols].rearrange("r (u p e) -> r u p e", u=2, e=2),
@@ -192,8 +211,8 @@ def tile_gated_vector_neuron_relu_s3_kernel(
             )
 
         def h_quant(i):
-            hq[i] = work.tile([P, 2 * P], U32, name="hq", tag="hq", bufs=2, align_bytes=256)
-            hs[i] = work.tile([P, 2 * P], U8, name="hs", tag="hs", bufs=2, align_bytes=256)
+            hq[i] = work.tile([P, 2 * P], U32, name="hq", tag="hq", bufs=3, align_bytes=256)
+            hs[i] = work.tile([P, 2 * P], U8, name="hs", tag="hs", bufs=3, align_bytes=256)
             nc.vector.quantize_mx(out=hq[i][:].bitcast(FP8X4), scales=hs[i][:], in_=hg[i][:])
 
         fbank, dbank, fsb, dsb, prod, summ, qt = {}, {}, {}, {}, {}, {}, {}
@@ -252,61 +271,93 @@ def tile_gated_vector_neuron_relu_s3_kernel(
             lift(i, 0, (0, 1))
             lift(i, 1, (0, 1))
         wg_copy(0)
-        wg_copy(1)
         wg_quant(0)
         lift(0, 0, (2,))
+        wg_copy(1)
         wg_quant(1)
-        lift(0, 1, (2,))
-        gate_mul(0, 0)
-        gate_mul(0, 1)
         x_transpose(2, FEAT)
         x_transpose(2, GEO)
         x_copy(2, FEAT)
         x_copy(2, GEO)
+        gate_mul(0, 0)
+        lift(0, 1, (2,))
+        gate_mul(0, 1)
         x_quant(2, FEAT)
         x_quant(2, GEO)
 
+        def ok(k):
+            return 0 <= k < TILES
+
         for i in range(TILES):
             j = i + AHEAD
-            if j < TILES:
+            b = i + 1
+            k = i
+            e = k - 1
+            if ok(j):
                 x_transpose(j, FEAT)
-            h_transpose(i)
-            if j < TILES:
+            if ok(i):
+                h_transpose(i)
+            if ok(j):
                 x_transpose(j, GEO)
                 x_copy(j, FEAT)
-            h_copy(i)
-            if j < TILES:
+            if ok(i):
+                h_copy(i)
+            if ok(j):
                 x_copy(j, GEO)
-            h_quant(i)
-            if i > 0:
-                product(i - 1)
-                d_copy(i - 1)
-            if i + 1 < TILES:
-                lift(i + 1, 0, (2,) if i == 0 else (0, 1, 2))
-                gate_mul(i + 1, 0)
-            if i > 0:
-                inner_sum(i - 1)
-            if i + 1 < TILES:
-                lift(i + 1, 1, (2,) if i == 0 else (0, 1, 2))
-                gate_mul(i + 1, 1)
-            if i >= V:
-                correction(i - V)
-            if j < TILES:
+            if ok(j + 1):
+                x_reorder(j + 1)
+            if ok(i):
+                h_quant(i)
+            if ok(e):
+                product(e)
+                d_copy(e)
+            if ok(b):
+                lift(b, 0, (2,) if b < 2 else (0, 1, 2))
+                gate_mul(b, 0)
+            if ok(e):
+                inner_sum(e)
+            if ok(b):
+                lift(b, 1, (2,) if b < 2 else (0, 1, 2))
+                gate_mul(b, 1)
+            if ok(e - 2):
+                correction(e - 2)
+            if ok(j):
                 x_quant(j, FEAT)
                 x_quant(j, GEO)
-            if i >= V:
-                finish(i - V)
-            project(i, wv, wv_s, fbank)
-            project(i, wd, wd_s, dbank)
-            f_copy(i)
+            if ok(e - 2):
+                finish(e - 2)
+            if ok(k):
+                project(k, wv, wv_s, fbank)
+                project(k, wd, wd_s, dbank)
+                f_copy(k)
 
         last = TILES - 1
+        m = last // V
+        rows = slice(m * P, (m + 1) * P)
         product(last)
-        d_copy(last)
-        inner_sum(last)
-        correction(last - 2)
-        correction(last - 1)
-        finish(last - 2)
-        correction(last)
-        finish(last - 1)
-        finish(last)
+        summ_last = work.tile([P, N], F32, name="summ", tag="summ", bufs=3)
+        nc.vector.tensor_tensor(out=summ_last[:], in0=summ[m][:], in1=prod[last][:], op=ALU.add)
+        neg_last = work.tile([P, N], F32, name="neg", tag="neg", bufs=2)
+        nc.scalar.activation(out=neg_last[:], in_=summ_last[:], func=ACT.Relu, scale=-1.0)
+        qg = work.tile([P, N], F32, name="qt", tag="qt", bufs=3)
+        nc.gpsimd.tensor_tensor(out=qg[:], in0=neg_last[:], in1=dsb[last - 2][:], op=ALU.mult)
+
+        def corr(i, d):
+            qt[i] = work.tile([P, N], F32, name="qt", tag="qt", bufs=3)
+            nc.vector.scalar_tensor_tensor(
+                out=qt[i][:], in0=summ_last[:], scalar=0.0, in1=d[:], op0=ALU.min, op1=ALU.mult,
+            )
+
+        def fin(i, f, qv, op, parts=1):
+            res = work.tile([P, N], F32, name="res", tag="res", bufs=3)
+            w = N // parts
+            for c in range(parts):
+                cols = slice(c * w, (c + 1) * w)
+                nc.vector.tensor_tensor(out=res[:, cols], in0=f[:, cols], in1=qv[:, cols], op=op)
+                nc.sync.dma_start(out=out[i % V, rows, cols], in_=res[:, cols])
+
+        corr(last, dbank[last])
+        corr(last - 1, dbank[last - 1])
+        fin(last, fbank[last], qt[last], ALU.subtract)
+        fin(last - 1, fbank[last - 1], qt[last - 1], ALU.subtract)
+        fin(last - 2, fsb[last - 2], qg, ALU.add, 1)

@@ -36,6 +36,9 @@ def tile_gated_vector_neuron_relu_s3_kernel(
         def bank():
             return psum.tile([P, BANK], F32, name="bank", tag="bank")
 
+        ident = keep.tile([P, P], F32, name="ident")
+        make_identity(nc, ident[:])
+
         wf = keep.tile([P, 2, 2 * H], U8, name="wf", align_bytes=256)
         wf_s = keep.tile([P, 2, H], U8, name="wf_s", align_bytes=256)
         wv = keep.tile([P, 2, 2 * N], U8, name="wv", align_bytes=256)
@@ -79,22 +82,19 @@ def tile_gated_vector_neuron_relu_s3_kernel(
         load_x(0, 1, 2)
         load_wg(0)
         load_wg(1)
-        load_gate(0)
         load_x(0, 2, 3)
+        load_gate(0)
         load_x(1, 0, 1)
+        load_scales(nc.sync, wv_s, w_val_scales)
         load_words(wv, w_val_words)
-        load_words(wd, w_dir_words)
-        load_scales(nc.gpsimd, wv_s, w_val_scales)
-        load_scales(nc.gpsimd, wd_s, w_dir_scales)
         load_x(1, 1, 2)
+        load_scales(nc.sync, wd_s, w_dir_scales)
+        load_words(wd, w_dir_words)
         load_gate(1)
         load_x(1, 2, 3)
         for m in range(2, POINTS // P):
             load_x(m, 0, V)
             load_gate(m)
-
-        ident = keep.tile([P, P], F32, name="ident")
-        make_identity(nc, ident[:])
 
         xq, xs, xg = {}, {}, {}
         xbank = {}

@@ -18,6 +18,9 @@ P = 128
 BANK = 512
 TILES = V * POINTS // P
 AHEAD = 3
+PASSES = (2, 0, 1)
+ADD_GP = (1, 2, 4, 5, 7, 8)
+Q_GP = ()
 
 FLOPS = 2 * V * POINTS * (KA + KB) * H + 2 * 2 * V * POINTS * H * N
 
@@ -77,19 +80,19 @@ def tile_gated_vector_neuron_relu_s3_kernel(
         for plane in (wf_s, wv_s, wd_s):
             nc.vector.memset(plane[:].bitcast(I32), 0)
         load_x(0, 0, 1)
+        load_wg(0)
         load_scales(nc.sync, wf_s, w_feat_scales)
+        load_wg(1)
         load_words(wf, w_feat_words)
         load_x(0, 1, 2)
-        load_wg(0)
-        load_wg(1)
-        load_x(0, 2, 3)
         load_gate(0)
-        load_x(1, 0, 1)
+        load_x(0, 2, 3)
         load_scales(nc.sync, wv_s, w_val_scales)
         load_words(wv, w_val_words)
-        load_x(1, 1, 2)
+        load_x(1, 0, 1)
         load_scales(nc.sync, wd_s, w_dir_scales)
         load_words(wd, w_dir_words)
+        load_x(1, 1, 2)
         load_gate(1)
         load_x(1, 2, 3)
         for m in range(2, POINTS // P):
@@ -181,7 +184,7 @@ def tile_gated_vector_neuron_relu_s3_kernel(
                     lhsT=xq[i][:, s * P:(s + 1) * P].bitcast(FP8X4),
                     lhsT_scale=xs[i][:, s * P:(s + 1) * P],
                     rhs=rhs, rhs_scale=rhs_scale,
-                    start=(s == 0), stop=(s == 2),
+                    start=(s == PASSES[0]), stop=(s == PASSES[-1]),
                 )
 
         hsb, hbank, hg, hq, hs = {}, {}, {}, {}, {}
@@ -246,10 +249,19 @@ def tile_gated_vector_neuron_relu_s3_kernel(
                 return
             left = prod[i - 1] if v == 1 else summ[m]
             summ[m] = work.tile([P, N], F32, name="summ", tag="summ", bufs=3)
-            nc.vector.tensor_tensor(out=summ[m][:], in0=left[:], in1=prod[i][:], op=ALU.add)
+            eng = nc.gpsimd if i in ADD_GP else nc.vector
+            eng.tensor_tensor(out=summ[m][:], in0=left[:], in1=prod[i][:], op=ALU.add)
+            if v == 2 and (i in Q_GP or i - 1 in Q_GP or i - 2 in Q_GP):
+                neg[m] = work.tile([P, N], F32, name="neg", tag="neg", bufs=2)
+                nc.scalar.activation(out=neg[m][:], in_=summ[m][:], func=ACT.Relu, scale=-1.0)
+
+        neg = {}
 
         def correction(i):
             qt[i] = work.tile([P, N], F32, name="qt", tag="qt", bufs=3)
+            if i in Q_GP:
+                nc.gpsimd.tensor_tensor(out=qt[i][:], in0=neg[i // V][:], in1=dsb[i][:], op=ALU.mult)
+                return
             nc.vector.scalar_tensor_tensor(
                 out=qt[i][:], in0=summ[i // V][:], scalar=0.0, in1=dsb[i][:], op0=ALU.min, op1=ALU.mult,
             )
@@ -257,31 +269,40 @@ def tile_gated_vector_neuron_relu_s3_kernel(
         def finish(i):
             m, v = divmod(i, V)
             res = work.tile([P, N], F32, name="res", tag="res", bufs=3)
-            nc.vector.tensor_tensor(out=res[:], in0=fsb[i][:], in1=qt[i][:], op=ALU.subtract)
+            nc.vector.tensor_tensor(out=res[:], in0=fsb[i][:], in1=qt[i][:], op=ALU.add if i in Q_GP else ALU.subtract)
             nc.sync.dma_start(out=out[v, m * P:(m + 1) * P, :], in_=res[:])
 
-        for i in range(2):
-            x_transpose(i, FEAT)
-            x_transpose(i, GEO)
-            x_copy(i, FEAT)
-            x_copy(i, GEO)
-            x_quant(i, FEAT)
-            x_quant(i, GEO)
-        for i in range(2):
-            lift(i, 0, (0, 1))
-            lift(i, 1, (0, 1))
+        def warm_up(n):
+            b = bank()
+            for r in range(n):
+                nc.tensor.matmul(b[:, 0:P], lhsT=ident[:], rhs=ident[:], start=True, stop=True)
+
+        warm_up(3)
+        x_transpose(0, FEAT)
+        x_transpose(0, GEO)
+        warm_up(4)
+        x_copy(0, FEAT)
+        x_copy(0, GEO)
         wg_copy(0)
+        x_quant(0, FEAT)
         wg_quant(0)
-        lift(0, 0, (2,))
+        x_quant(0, GEO)
         wg_copy(1)
         wg_quant(1)
+        lift(0, 0, PASSES)
+        x_transpose(1, FEAT)
+        x_transpose(1, GEO)
+        x_copy(1, FEAT)
+        x_copy(1, GEO)
+        lift(0, 1, PASSES)
         x_transpose(2, FEAT)
         x_transpose(2, GEO)
+        gate_mul(0, 0)
+        x_quant(1, FEAT)
+        gate_mul(0, 1)
+        x_quant(1, GEO)
         x_copy(2, FEAT)
         x_copy(2, GEO)
-        gate_mul(0, 0)
-        lift(0, 1, (2,))
-        gate_mul(0, 1)
         x_quant(2, FEAT)
         x_quant(2, GEO)
 
@@ -312,12 +333,12 @@ def tile_gated_vector_neuron_relu_s3_kernel(
                 product(e)
                 d_copy(e)
             if ok(b):
-                lift(b, 0, (2,) if b < 2 else (0, 1, 2))
+                lift(b, 0, PASSES)
                 gate_mul(b, 0)
             if ok(e):
                 inner_sum(e)
             if ok(b):
-                lift(b, 1, (2,) if b < 2 else (0, 1, 2))
+                lift(b, 1, PASSES)
                 gate_mul(b, 1)
             if ok(e - 2):
                 correction(e - 2)

@@ -87,14 +87,14 @@ def tile_gated_vector_neuron_relu_s3_kernel(
         load_x(0, 1, 2)
         load_gate(0)
         load_x(0, 2, 3)
-        load_scales(nc.sync, wv_s, w_val_scales)
         load_words(wv, w_val_words)
         load_x(1, 0, 1)
-        load_scales(nc.sync, wd_s, w_dir_scales)
         load_words(wd, w_dir_words)
         load_x(1, 1, 2)
         load_gate(1)
         load_x(1, 2, 3)
+        load_scales(nc.gpsimd, wv_s, w_val_scales)
+        load_scales(nc.gpsimd, wd_s, w_dir_scales)
         for m in range(2, POINTS // P):
             load_x(m, 0, V)
             load_gate(m)
@@ -314,16 +314,13 @@ def tile_gated_vector_neuron_relu_s3_kernel(
             b = i + 1
             k = i
             e = k - 1
+            h_transpose(i)
             if ok(j):
                 x_transpose(j, FEAT)
-            if ok(i):
-                h_transpose(i)
-            if ok(j):
                 x_transpose(j, GEO)
-                x_copy(j, FEAT)
-            if ok(i):
-                h_copy(i)
+            h_copy(i)
             if ok(j):
+                x_copy(j, FEAT)
                 x_copy(j, GEO)
             if ok(j + 1):
                 x_reorder(j + 1)
@@ -331,7 +328,6 @@ def tile_gated_vector_neuron_relu_s3_kernel(
                 h_quant(i)
             if ok(e):
                 product(e)
-                d_copy(e)
             if ok(b):
                 lift(b, 0, PASSES)
                 gate_mul(b, 0)
@@ -351,6 +347,8 @@ def tile_gated_vector_neuron_relu_s3_kernel(
                 project(k, wv, wv_s, fbank)
                 project(k, wd, wd_s, dbank)
                 f_copy(k)
+                if k < TILES - 1:
+                    d_copy(k)
 
         last = TILES - 1
         m = last // V

from contextlib import ExitStack

import concourse.mybir as mybir
from concourse.masks import make_identity

F32 = mybir.dt.float32
BF16 = mybir.dt.bfloat16
U32 = mybir.dt.uint32
I32 = mybir.dt.int32
U8 = mybir.dt.uint8
FP8X4 = mybir.dt.float8_e4m3fn_x4
FP4X4 = mybir.dt.float4_e2m1fn_x4
ALU = mybir.AluOpType
ACT = mybir.ActivationFunctionType

V, POINTS, KA, KB, H, N = 3, 512, 512, 1024, 1024, 512
P = 128
BANK = 512
TILES = V * POINTS // P
AHEAD = 3
PASSES = (2, 0, 1)
ADD_GP = (1, 2, 4, 5, 7, 8)
Q_GP = ()

FLOPS = 2 * V * POINTS * (KA + KB) * H + 2 * 2 * V * POINTS * H * N


def tile_gated_vector_neuron_relu_s3_kernel(
    tc, x_geo, x_feat, w_geo, w_feat_words, w_feat_scales, gate,
    w_val_words, w_val_scales, w_dir_words, w_dir_scales, out,
):
    nc = tc.nc
    with ExitStack() as ctx:
        ctx.enter_context(tc.manual_schedule())
        keep = ctx.enter_context(tc.tile_pool(name="keep", bufs=1))
        work = ctx.enter_context(tc.tile_pool(name="work", bufs=2))
        psum = ctx.enter_context(tc.psum_pool(name="psum", bufs=8))

        def bank():
            return psum.tile([P, BANK], F32, name="bank", tag="bank")

        ident = keep.tile([P, P], F32, name="ident")
        make_identity(nc, ident[:])

        wf = keep.tile([P, 2, 2 * H], U8, name="wf", align_bytes=256)
        wf_s = keep.tile([P, 2, H], U8, name="wf_s", align_bytes=256)
        wv = keep.tile([P, 2, 2 * N], U8, name="wv", align_bytes=256)
        wv_s = keep.tile([P, 2, N], U8, name="wv_s", align_bytes=256)
        wd = keep.tile([P, 2, 2 * N], U8, name="wd", align_bytes=256)
        wd_s = keep.tile([P, 2, N], U8, name="wd_s", align_bytes=256)
        wg_raw = [keep.tile([P, 4, BANK], BF16, name=f"wg_raw{h}", align_bytes=256) for h in range(2)]
        x_sb = [keep.tile([P, V, KB + KA], BF16, name=f"x{m}", align_bytes=256) for m in range(POINTS // P)]
        gate_sb = [keep.tile([P, H], BF16, name=f"gate{m}", align_bytes=256) for m in range(POINTS // P)]

        def load_x(m, v0, v1):
            for x, cols in ((x_feat, slice(0, KB)), (x_geo, slice(KB, KB + KA))):
                rows = x.rearrange("(v q) k -> q v k", v=V)
                nc.sync.dma_start(out=x_sb[m][:, v0:v1, cols], in_=rows[m * P:(m + 1) * P, v0:v1, :])

        def load_gate(m):
            nc.sync.dma_start(out=gate_sb[m][:], in_=gate[m * P:(m + 1) * P, :])

        def load_words(tile, words):
            nc.sync.dma_start(out=tile[:].bitcast(I32), in_=words.bitcast(I32).rearrange("g p b -> p g b"))

        def load_scales(queue, tile, scales):
            src = scales.bitcast(I32)
            for q in range(4):
                queue.dma_start(
                    out=tile[32 * q:32 * q + 4, :, :].bitcast(I32),
                    in_=src[:, 4 * q:4 * q + 4, :].rearrange("g q n -> q g n"),
                )

        def load_wg(h):
            nc.sync.dma_start(
                out=wg_raw[h][:],
                in_=w_geo.rearrange("(p j) c -> p j c", j=4)[:, :, h * BANK:(h + 1) * BANK],
            )

        for plane in (wf_s, wv_s, wd_s):
            nc.vector.memset(plane[:].bitcast(I32), 0)
        load_x(0, 0, 1)
        load_wg(0)
        load_scales(nc.sync, wf_s, w_feat_scales)
        load_wg(1)
        load_words(wf, w_feat_words)
        load_x(0, 1, 2)
        load_gate(0)
        load_x(0, 2, 3)
        load_words(wv, w_val_words)
        load_x(1, 0, 1)
        load_words(wd, w_dir_words)
        load_x(1, 1, 2)
        load_gate(1)
        load_x(1, 2, 3)
        load_scales(nc.gpsimd, wv_s, w_val_scales)
        load_scales(nc.gpsimd, wd_s, w_dir_scales)
        for m in range(2, POINTS // P):
            load_x(m, 0, V)
            load_gate(m)

        xq, xs, xg = {}, {}, {}
        xbank = {}

        xr = {}

        def x_reorder(i):
            xr[i] = work.tile([P, KB + KA], BF16, name="xr", tag="xr", bufs=2, align_bytes=256)
            nc.scalar.copy(
                out=xr[i][:].bitcast(F32).rearrange("p (g u w) -> p g u w", g=3, u=2),
                in_=x_sb[i // V][:, i % V, :].bitcast(F32).rearrange("p (g w u) -> p g u w", g=3, u=2),
            )

        def x_transpose(i, passes):
            b = bank()
            slot = 0
            for g in passes:
                for u in range(2):
                    if i in xr:
                        words = xr[i][:].bitcast(F32)[:, 256 * g + 128 * u:256 * g + 128 * (u + 1)]
                    else:
                        words = x_sb[i // V][:, i % V, :].bitcast(F32)[:, 256 * g + u:256 * (g + 1):2]
                    nc.tensor.transpose(b[:, slot * P:(slot + 1) * P], words, ident[:])
                    slot += 1
            xbank[i, passes] = b

        def x_copy(i, passes):
            if i not in xg:
                xg[i] = work.tile([P, 3 * 4 * P], BF16, name="xg", tag="xg", bufs=3, align_bytes=256)
            n = len(passes)
            c0 = passes[0] * 4 * P
            dst = xg[i][:, c0:c0 + n * 4 * P].bitcast(F32).rearrange("p (g r u) -> p g r u", g=n, u=2)
            src = xbank[i, passes][:, 0:n * 2 * P].rearrange("p (g u r) -> p g r u", g=n, u=2)
            nc.scalar.copy(out=dst, in_=src)

        def x_quant(i, passes):
            if i not in xq:
                xq[i] = work.tile([P, 3 * P], U32, name="xq", tag="xq", bufs=AHEAD + 2, align_bytes=256)
                xs[i] = work.tile([P, 3 * P], U8, name="xs", tag="xs", bufs=AHEAD + 2, align_bytes=256)
            n = len(passes)
            c0 = passes[0] * P
            nc.vector.quantize_mx(
                out=xq[i][:, c0:c0 + n * P].bitcast(FP8X4),
                scales=xs[i][:, c0:c0 + n * P],
                in_=xg[i][:, 4 * c0:4 * (c0 + n * P)],
            )

        FEAT, GEO = (0, 1), (2,)

        wg_codes = keep.tile([P, H], U32, name="wg_codes", align_bytes=256)
        wg_scales = keep.tile([P, H], U8, name="wg_scales", align_bytes=256)
        wg_grp = [keep.tile([P, BANK, 4], BF16, name=f"wg_grp{h}", align_bytes=256) for h in range(2)]

        def wg_copy(h):
            half = BANK // 2
            for copy, c0 in ((nc.vector.tensor_copy, 0), (nc.scalar.copy, half)):
                copy(
                    out=wg_grp[h][:, c0:c0 + half, :].rearrange("p (c i) t -> p c t i", i=4),
                    in_=wg_raw[h][:, :, c0:c0 + half].rearrange("p t (c i) -> p c t i", i=4),
                )

        def wg_quant(h):
            cols = slice(h * BANK, (h + 1) * BANK)
            nc.vector.quantize_mx(
                out=wg_codes[:, cols].bitcast(FP8X4), scales=wg_scales[:, cols],
                in_=wg_grp[h][:].rearrange("p c t -> p (c t)"),
            )

        z = {}

        def lift(i, h, parts):
            cols = slice(h * BANK, (h + 1) * BANK)
            if (i, h) not in z:
                z[i, h] = bank()
            for s in parts:
                if s < 2:
                    rhs = wf[:, s, 2 * h * BANK:2 * (h + 1) * BANK].bitcast(FP4X4)
                    rhs_scale = wf_s[:, s, cols]
                else:
                    rhs = wg_codes[:, cols].bitcast(FP8X4)
                    rhs_scale = wg_scales[:, cols]
                nc.tensor.matmul_mx(
                    out=z[i, h][:],
                    lhsT=xq[i][:, s * P:(s + 1) * P].bitcast(FP8X4),
                    lhsT_scale=xs[i][:, s * P:(s + 1) * P],
                    rhs=rhs, rhs_scale=rhs_scale,
                    start=(s == PASSES[0]), stop=(s == PASSES[-1]),
                )

        hsb, hbank, hg, hq, hs = {}, {}, {}, {}, {}

        def gate_mul(i, h):
            if i not in hsb:
                hsb[i] = work.tile([P, H], BF16, name="hsb", tag="hsb", bufs=4, align_bytes=256)
            cols = slice(h * BANK, (h + 1) * BANK)
            nc.vector.tensor_tensor(
                out=hsb[i][:, cols].rearrange("r (u p e) -> r u p e", u=2, e=2),
                in0=z[i, h][:].rearrange("r (p u e) -> r u p e", u=2, e=2),
                in1=gate_sb[i // V][:, cols].rearrange("r (p u e) -> r u p e", u=2, e=2),
                op=ALU.mult,
            )

        def h_transpose(i):
            hbank[i] = bank()
            words = hsb[i][:].bitcast(F32)
            for s in range(4):
                nc.tensor.transpose(hbank[i][:, s * P:(s + 1) * P], words[:, s * P:(s + 1) * P], ident[:])

        def h_copy(i):
            hg[i] = work.tile([P, 2 * 4 * P], BF16, name="hg", tag="hg", bufs=2, align_bytes=256)
            nc.scalar.copy(
                out=hg[i][:].bitcast(F32).rearrange("p (g r u) -> p g r u", g=2, u=2),
                in_=hbank[i][:].rearrange("p (g u r) -> p g r u", g=2, u=2),
            )

        def h_quant(i):
            hq[i] = work.tile([P, 2 * P], U32, name="hq", tag="hq", bufs=3, align_bytes=256)
            hs[i] = work.tile([P, 2 * P], U8, name="hs", tag="hs", bufs=3, align_bytes=256)
            nc.vector.quantize_mx(out=hq[i][:].bitcast(FP8X4), scales=hs[i][:], in_=hg[i][:])

        fbank, dbank, fsb, dsb, prod, summ, qt = {}, {}, {}, {}, {}, {}, {}

        def project(i, w, w_s, banks):
            banks[i] = bank()
            for g in range(2):
                nc.tensor.matmul_mx(
                    out=banks[i][:],
                    lhsT=hq[i][:, g * P:(g + 1) * P].bitcast(FP8X4),
                    lhsT_scale=hs[i][:, g * P:(g + 1) * P],
                    rhs=w[:, g, :].bitcast(FP4X4), rhs_scale=w_s[:, g, :],
                    start=(g == 0), stop=(g == 1),
                )

        def f_copy(i):
            fsb[i] = work.tile([P, N], F32, name="fsb", tag=f"f{i % V}", bufs=2)
            nc.scalar.copy(out=fsb[i][:], in_=fbank[i][:])

        def d_copy(i):
            dsb[i] = work.tile([P, N], F32, name="dsb", tag=f"d{i % V}", bufs=2)
            nc.scalar.copy(out=dsb[i][:], in_=dbank[i][:])

        def product(i):
            prod[i] = work.tile([P, N], F32, name="prod", tag="prod", bufs=3)
            nc.vector.tensor_tensor(out=prod[i][:], in0=dbank[i][:], in1=fsb[i][:], op=ALU.mult)

        def inner_sum(i):
            m, v = divmod(i, V)
            if v == 0:
                return
            left = prod[i - 1] if v == 1 else summ[m]
            summ[m] = work.tile([P, N], F32, name="summ", tag="summ", bufs=3)
            eng = nc.gpsimd if i in ADD_GP else nc.vector
            eng.tensor_tensor(out=summ[m][:], in0=left[:], in1=prod[i][:], op=ALU.add)
            if v == 2 and (i in Q_GP or i - 1 in Q_GP or i - 2 in Q_GP):
                neg[m] = work.tile([P, N], F32, name="neg", tag="neg", bufs=2)
                nc.scalar.activation(out=neg[m][:], in_=summ[m][:], func=ACT.Relu, scale=-1.0)

        neg = {}

        def correction(i):
            qt[i] = work.tile([P, N], F32, name="qt", tag="qt", bufs=3)
            if i in Q_GP:
                nc.gpsimd.tensor_tensor(out=qt[i][:], in0=neg[i // V][:], in1=dsb[i][:], op=ALU.mult)
                return
            nc.vector.scalar_tensor_tensor(
                out=qt[i][:], in0=summ[i // V][:], scalar=0.0, in1=dsb[i][:], op0=ALU.min, op1=ALU.mult,
            )

        def finish(i):
            m, v = divmod(i, V)
            res = work.tile([P, N], F32, name="res", tag="res", bufs=3)
            nc.vector.tensor_tensor(out=res[:], in0=fsb[i][:], in1=qt[i][:], op=ALU.add if i in Q_GP else ALU.subtract)
            nc.sync.dma_start(out=out[v, m * P:(m + 1) * P, :], in_=res[:])

        def warm_up(n):
            b = bank()
            for r in range(n):
                nc.tensor.matmul(b[:, 0:P], lhsT=ident[:], rhs=ident[:], start=True, stop=True)

        warm_up(3)
        x_transpose(0, FEAT)
        x_transpose(0, GEO)
        warm_up(4)
        x_copy(0, FEAT)
        x_copy(0, GEO)
        wg_copy(0)
        x_quant(0, FEAT)
        wg_quant(0)
        x_quant(0, GEO)
        wg_copy(1)
        wg_quant(1)
        lift(0, 0, PASSES)
        x_transpose(1, FEAT)
        x_transpose(1, GEO)
        x_copy(1, FEAT)
        x_copy(1, GEO)
        lift(0, 1, PASSES)
        x_transpose(2, FEAT)
        x_transpose(2, GEO)
        gate_mul(0, 0)
        x_quant(1, FEAT)
        gate_mul(0, 1)
        x_quant(1, GEO)
        x_copy(2, FEAT)
        x_copy(2, GEO)
        x_quant(2, FEAT)
        x_quant(2, GEO)

        def ok(k):
            return 0 <= k < TILES

        for i in range(TILES):
            j = i + AHEAD
            b = i + 1
            k = i
            e = k - 1
            h_transpose(i)
            if ok(j):
                x_transpose(j, FEAT)
                x_transpose(j, GEO)
            h_copy(i)
            if ok(j):
                x_copy(j, FEAT)
                x_copy(j, GEO)
            if ok(j + 1):
                x_reorder(j + 1)
            if ok(i):
                h_quant(i)
            if ok(e):
                product(e)
            if ok(b):
                lift(b, 0, PASSES)
                gate_mul(b, 0)
            if ok(e):
                inner_sum(e)
            if ok(b):
                lift(b, 1, PASSES)
                gate_mul(b, 1)
            if ok(e - 2):
                correction(e - 2)
            if ok(j):
                x_quant(j, FEAT)
                x_quant(j, GEO)
            if ok(e - 2):
                finish(e - 2)
            if ok(k):
                project(k, wv, wv_s, fbank)
                project(k, wd, wd_s, dbank)
                f_copy(k)
                if k < TILES - 1:
                    d_copy(k)

        last = TILES - 1
        m = last // V
        rows = slice(m * P, (m + 1) * P)
        product(last)
        summ_last = work.tile([P, N], F32, name="summ", tag="summ", bufs=3)
        nc.vector.tensor_tensor(out=summ_last[:], in0=summ[m][:], in1=prod[last][:], op=ALU.add)
        neg_last = work.tile([P, N], F32, name="neg", tag="neg", bufs=2)
        nc.scalar.activation(out=neg_last[:], in_=summ_last[:], func=ACT.Relu, scale=-1.0)
        qg = work.tile([P, N], F32, name="qt", tag="qt", bufs=3)
        nc.gpsimd.tensor_tensor(out=qg[:], in0=neg_last[:], in1=dsb[last - 2][:], op=ALU.mult)

        def corr(i, d):
            qt[i] = work.tile([P, N], F32, name="qt", tag="qt", bufs=3)
            nc.vector.scalar_tensor_tensor(
                out=qt[i][:], in0=summ_last[:], scalar=0.0, in1=d[:], op0=ALU.min, op1=ALU.mult,
            )

        def fin(i, f, qv, op, parts=1):
            res = work.tile([P, N], F32, name="res", tag="res", bufs=3)
            w = N // parts
            for c in range(parts):
                cols = slice(c * w, (c + 1) * w)
                nc.vector.tensor_tensor(out=res[:, cols], in0=f[:, cols], in1=qv[:, cols], op=op)
                nc.sync.dma_start(out=out[i % V, rows, cols], in_=res[:, cols])

        corr(last, dbank[last])
        corr(last - 1, dbank[last - 1])
        fin(last, fbank[last], qt[last], ALU.subtract)
        fin(last - 1, fbank[last - 1], qt[last - 1], ALU.subtract)
        fin(last - 2, fsb[last - 2], qg, ALU.add, 1)
